import numpy as np
import ml_dtypes


def mxq(x, axis, fmt="e4m3"):
    dtype, down = {"e4m3": (ml_dtypes.float8_e4m3fn, 7), "e5m2": (ml_dtypes.float8_e5m2, 14)}[fmt]
    v = np.moveaxis(np.asarray(x, np.float32).astype(ml_dtypes.bfloat16).astype(np.float64), axis, -1)
    blocks = v.reshape(v.shape[:-1] + (-1, 32))
    amax = np.abs(blocks).max(-1, keepdims=True)
    byte = np.maximum(np.where(amax > 0, np.frexp(amax)[1] - 1 + 127, 0) - down, 1)
    scale = np.exp2(byte - 127.0)
    codes = (blocks / scale).astype(np.float32).astype(dtype).astype(np.float64)
    return np.moveaxis((codes * scale).reshape(v.shape), -1, axis)


WIDE = False


def mx_kscale(k):
    if not WIDE:
        return np.ones(k)
    levels = np.array([10, -10, 5, -5, 0])
    if k % 512:
        return np.exp2(np.random.permutation(np.resize(levels, k // 32))).repeat(32)
    a = np.empty((k // 512, 16))
    for p in range(k // 512):
        a[p, :8] = np.random.permutation(np.resize(levels, 8))
        for g in range(8):
            far = levels[np.abs(levels - a[p, g]) >= 10]
            a[p, g + 8] = far[np.random.randint(len(far))]
    return np.exp2(a.ravel()).repeat(32)


def f64(x):
    return np.asarray(x).astype(np.float64)


def striped(idx):
    return np.tile(idx.reshape(-1, 16).T, (8, 1)).astype(np.uint16)


def unstriped(offs):
    return offs[:16].T.reshape(-1).astype(np.int64)


E2M1 = np.array([0.0, 0.5, 1.0, 1.5, 2.0, 3.0, 4.0, 6.0, -0.0, -0.5, -1.0, -1.5, -2.0, -3.0, -4.0, -6.0])


def pack_weight(w, fmt):
    k, n = w.shape
    w = f64(np.asarray(w, np.float32).astype(ml_dtypes.bfloat16)).reshape(k // 32, 32, n)
    amax = np.abs(w).max(1)
    if fmt == "e4m3":
        byte = np.frexp(amax)[1] - 1 + 127 - 7
    else:
        mant, ex = np.frexp(amax / 6.0)
        byte = np.where(mant > 0.5, ex, ex - 1) + 127
    byte = np.clip(np.where(amax > 0, byte, 1), 1, 254)
    scaled = (w * np.exp2(127.0 - byte)[:, None, :]).reshape(k, n).astype(np.float32)
    by_word = np.ascontiguousarray(scaled.reshape(k // 512, 128, 4, n).transpose(0, 1, 3, 2))
    if fmt == "e4m3":
        words = by_word.astype(ml_dtypes.float8_e4m3fn).view(np.uint8)
    else:
        c = by_word.astype(ml_dtypes.float4_e2m1fn).view(np.uint8) & 0xF
        words = (c[..., 0::2] | (c[..., 1::2] << 4)).reshape(k // 512, 128, 2 * n)
    return np.ascontiguousarray(words), np.ascontiguousarray(byte.astype(np.uint8).reshape(k // 512, 16, n))


def unpack_weight(words, scales, fmt):
    g, _, n = scales.shape
    words = np.ascontiguousarray(words).reshape(g, 128, n, -1)
    if fmt == "e4m3":
        vals = words.view(ml_dtypes.float8_e4m3fn).astype(np.float64)
    else:
        nib = np.empty((g, 128, n, 4), np.uint8)
        nib[..., 0::2] = words & 0xF
        nib[..., 1::2] = words >> 4
        vals = E2M1[nib]
    vals = vals * np.repeat(np.exp2(scales.astype(np.float64) - 127.0), 8, axis=1)[..., None]
    return vals.transpose(0, 1, 3, 2).reshape(g * 512, n)


def gelu(v):
    return 0.5 * v * (1.0 + np.tanh(np.sqrt(2.0 / np.pi) * (v + 0.044715 * v**3)))


def bf(x):
    return np.asarray(x, np.float32).astype(ml_dtypes.bfloat16)


def planes(Y):
    n, m = Y.shape
    b = f64(bf(Y)).reshape(n // 32, 32, m)
    amax = np.abs(b).max(1)
    byte = np.clip(np.where(amax > 0, np.frexp(amax)[1] - 1 + 127 - 7, 1), 1, 254)
    codes = (b * np.exp2(127.0 - byte)[:, None, :]).reshape(n, m).astype(np.float32).astype(ml_dtypes.float8_e4m3fn).view(np.uint8)
    words = codes.reshape(n // 512, 128, 4, m).transpose(0, 1, 3, 2)
    return np.ascontiguousarray(words), np.ascontiguousarray(byte.astype(np.uint8).reshape(n // 512, 16, m))


K, T, S, P, H, N = 1024, 4096, 1024, 512, 1024, 512

def setup_inputs():
    n = np.random.standard_normal
    uni = np.random.uniform
    s = mx_kscale(K)[:, None]
    u = mx_kscale(H)[:, None]
    size = np.exp(0.8 * n(N))
    d = {}
    d["tab_words"], d["tab_scales"] = pack_weight(n((K, T)) * s, "e4m3")
    d["offs"] = striped(np.random.permutation(T)[:S])
    ends = np.random.permutation(S)
    d["pos1"] = striped(ends[:P])
    d["pos2"] = striped(ends[P:2 * P])
    d["w1"] = (n((K, H)) / K**0.5 / s).astype(np.float32)
    d["lo"] = (-uni(0.2, 1.5, H)).astype(np.float32)
    d["hi"] = uni(0.2, 1.5, H).astype(np.float32)
    d["gain"] = (np.exp(0.3 * n(H)) * u[:, 0]).astype(np.float32)
    d["w2_words"], d["w2_scales"] = pack_weight(2.2 * n((H, N)) / H**0.5 / u, "e2m1")
    d["w3"] = (0.9 * n((H, N)) / H**0.5 / u * size).astype(np.float32)
    d["base"] = (-(0.4 + 0.7 * size) * uni(0.3, 1.2, N)).astype(np.float32)
    return d

def reference(tab_words, tab_scales, offs, pos1, pos2, w1, lo, hi, gain, w2_words, w2_scales, w3, base):
    v = unpack_weight(tab_words, tab_scales, "e4m3")[:, unstriped(offs)]
    w2 = unpack_weight(w2_words, w2_scales, "e2m1")
    pores = mxq(f64(w1), 0, "e4m3").T @ v
    held = np.minimum(np.maximum(pores, f64(lo)[:, None]), f64(hi)[:, None])
    h = mxq(f64(gain)[:, None] * held, 0, "e4m3")
    bent = np.tanh(w2.T @ h)
    g2 = bent + (mxq(f64(w3), 0, "e4m3").T @ h)
    y = np.maximum(g2[:, unstriped(pos1)] - g2[:, unstriped(pos2)], f64(base)[:, None])
    words, scales = planes(y)
    return y, words, scales

@@ -1,0 +1,210 @@
+from contextlib import ExitStack
+
+import concourse.mybir as mybir
+
+K, T, S, PAIRS, H, N = 1024, 4096, 1024, 512, 1024, 512
+FLOPS = 2 * K * H * S + 2 * 2 * H * N * S
+
+F32 = mybir.dt.float32
+BF16 = mybir.dt.bfloat16
+I32 = mybir.dt.int32
+U32 = mybir.dt.uint32
+U16 = mybir.dt.uint16
+U8 = mybir.dt.uint8
+FP8X4 = mybir.dt.float8_e4m3fn_x4
+FP4X4 = mybir.dt.float4_e2m1fn_x4
+ALU = mybir.AluOpType
+ACT = mybir.ActivationFunctionType
+
+P = 128
+PACK = 4
+PASS = 512
+HALF = 512
+STAGE_DT = F32
+
+
+def tile_list_cork_end_contrast_kernel(tc, tab_words, tab_scales, offs, pos1, pos2, w1, lo, hi, gain,
+                                                 w2_words, w2_scales, w3, base, out_0, out_1, out_2):
+    nc = tc.nc
+    with ExitStack() as ctx:
+        keep = ctx.enter_context(tc.tile_pool(name="keep", bufs=1))
+        ring = ctx.enter_context(tc.tile_pool(name="ring", bufs=2))
+        psum = ctx.enter_context(tc.psum_pool(name="psum", bufs=8))
+
+        idx = keep.tile([P, S // 16], U16, name="idx")
+        p1 = keep.tile([P, PAIRS // 16], U16, name="p1")
+        p2 = keep.tile([P, PAIRS // 16], U16, name="p2")
+        tw = [keep.tile([P, T], I32, name="tw%d" % a, align_bytes=64) for a in range(2)]
+        ts = keep.tile([P, T], U8, name="ts", align_bytes=64)
+        w2w = keep.tile([P, 2, 2 * N], U8, name="w2w", align_bytes=64)
+        w2s = keep.tile([P, 2, N], U8, name="w2s", align_bytes=64)
+        w1raw = {(a, b): keep.tile([P, PACK, PASS], F32, name="w1raw%d%d" % (a, b)) for a in range(2) for b in range(2)}
+        w3raw = [keep.tile([P, PACK, N], F32, name="w3raw%d" % b) for b in range(2)]
+        lo_t = keep.tile([P, 2, PACK], F32, name="lo_t")
+        hi_t = keep.tile([P, 2, PACK], F32, name="hi_t")
+        gain_t = keep.tile([P, 2, PACK], F32, name="gain_t")
+        base_t = keep.tile([P, PACK], F32, name="base_t")
+
+        warm = keep.tile([P, 2], F32, name="warm")
+        nc.vector.memset(ts[:].bitcast(I32), 0)
+        nc.vector.memset(w2s[:].rearrange("p b n -> p (b n)").bitcast(I32), 0)
+        nc.vector.memset(warm[:, 0:1], 0.0)
+        nc.scalar.activation(warm[:, 1:2], warm[:, 0:1], ACT.Tanh)
+
+        def load_table(a):
+            nc.sync.dma_start(tw[a][:], tab_words[a].rearrange("p t i -> p (t i)").bitcast(I32))
+
+        def load_w1(a, b):
+            nc.sync.dma_start(w1raw[a, b][:], w1[PASS * a:PASS * (a + 1), PASS * b:PASS * (b + 1)].rearrange("(p j) c -> p j c", j=PACK))
+
+        def load_vec(queue, src, dst):
+            queue.dma_start(dst[:], src.rearrange("(b p t) -> p b t", b=2, t=PACK))
+
+        load_table(0)
+        for q in range(4):
+            nc.sync.dma_start(ts[32 * q:32 * q + 8, :].bitcast(I32), tab_scales[:, 4 * q:4 * q + 4, :].bitcast(I32))
+        nc.sync.dma_start(idx[:], offs)
+        load_w1(0, 0)
+        nc.sync.dma_start(w2w[:].bitcast(I32), w2_words.rearrange("b p c -> p b c").bitcast(I32))
+        load_table(1)
+        for q in range(4):
+            nc.sync.dma_start(w2s[32 * q:32 * q + 4, :, :].bitcast(I32), w2_scales[:, 4 * q:4 * q + 4, :].rearrange("b r n -> r b n").bitcast(I32))
+        load_w1(1, 0)
+        for src, dst in ((gain, gain_t), (lo, lo_t), (hi, hi_t)):
+            load_vec(nc.sync, src, dst)
+        load_w1(0, 1)
+        load_w1(1, 1)
+        for b in range(2):
+            nc.sync.dma_start(w3raw[b][:], w3[PASS * b:PASS * (b + 1), :].rearrange("(p j) c -> p j c", j=PACK))
+        nc.sync.dma_start(p1[:], pos1)
+        nc.sync.dma_start(p2[:], pos2)
+        nc.sync.dma_start(base_t[:], base.rearrange("(p t) -> p t", t=PACK))
+
+        vw = {(a, sh): keep.tile([P, HALF], U32, name="vw%d%d" % (a, sh), align_bytes=64) for a in range(2) for sh in range(2)}
+        vs = [keep.tile([P, HALF], U8, name="vs%d" % sh, align_bytes=64) for sh in range(2)]
+
+        def gather_words(a, sh):
+            nc.vector.tensor_copy(vw[a, sh][:], tw[a][:].bitcast(U32).indirect(idx[:, 32 * sh:32 * (sh + 1)]))
+
+        def gather_scales(sh):
+            nc.vector.tensor_copy(vs[sh][:], ts[:].indirect(idx[:, 32 * sh:32 * (sh + 1)]))
+
+        def cast_weight(raw, name, m_vec):
+            grouped = ring.tile([P, PACK * PASS], BF16, name="grouped", bufs=3, align_bytes=64)
+            dst = grouped[:].rearrange("p (t m j) -> p m j t", t=PACK, j=PACK)
+            src = raw[:].rearrange("p j (m t) -> p m j t", t=PACK)
+            if m_vec > 0:
+                nc.vector.tensor_copy(dst[:, 0:m_vec], src[:, 0:m_vec])
+            if m_vec < P:
+                nc.scalar.copy(dst[:, m_vec:P], src[:, m_vec:P])
+            return grouped
+
+        def quantise(grouped, name):
+            codes = keep.tile([P, PASS], U32, name="c" + name, align_bytes=64)
+            scales = keep.tile([P, PASS], U8, name="s" + name, align_bytes=64)
+            nc.vector.quantize_mx(out=codes[:].bitcast(FP8X4), scales=scales[:], in_=grouped[:])
+            return codes, scales
+
+        lo2 = keep.tile([P, 2, PACK], F32, name="lo2")
+        ea = keep.tile([P, 2, PACK], F32, name="ea")
+        eb = keep.tile([P, 2, PACK], F32, name="eb")
+        low = keep.tile([P, 2, PACK], F32, name="low")
+        upp = keep.tile([P, 2, PACK], F32, name="upp")
+        nc.vector.tensor_tensor(lo2[:], lo_t[:], hi_t[:], ALU.min)
+        nc.vector.tensor_tensor(eb[:], hi_t[:], gain_t[:], ALU.mult)
+        nc.vector.tensor_tensor(ea[:], lo2[:], gain_t[:], ALU.mult)
+        nc.vector.tensor_tensor(low[:], ea[:], eb[:], ALU.min)
+        nc.vector.tensor_tensor(upp[:], ea[:], eb[:], ALU.max)
+
+        w1q = {}
+        gather_words(0, 0)
+        gather_words(0, 1)
+        gather_scales(0)
+        gather_scales(1)
+        g00 = cast_weight(w1raw[0, 0], "w100", 0)
+        w2wd = keep.tile([P, 2, PACK, 2 * P], U8, name="w2wd", align_bytes=64)
+        w2sd = keep.tile([P, 2, PACK, P], U8, name="w2sd", align_bytes=64)
+        nc.vector.tensor_copy(w2wd[:].rearrange("p b t (q e) -> p b q t e", e=2), w2w[:].rearrange("p b (q t e) -> p b q t e", t=PACK, e=2))
+        w1q[0, 0] = quantise(g00, "w100")
+        nc.vector.tensor_copy(w2sd[:].rearrange("p b t q -> p b q t"), w2s[:].rearrange("p b (q t) -> p b q t", t=PACK))
+        gather_words(1, 0)
+        gather_words(1, 1)
+        w1q[1, 0] = quantise(cast_weight(w1raw[1, 0], "w110", 84), "w110")
+
+        hq = {}
+
+        def stage1(b, sh):
+            scaled = ring.tile([P, PACK, HALF], STAGE_DT, name="scaled")
+            held = ring.tile([P, PACK, HALF], BF16, name="held")
+            for t in range(PACK):
+                acc = psum.tile([P, HALF], F32, name="acc")
+                for a in range(2):
+                    codes, scales = w1q[a, b]
+                    nc.tensor.matmul_mx(out=acc[:], lhsT=codes[:, P * t:P * (t + 1)].bitcast(FP8X4), lhsT_scale=scales[:, P * t:P * (t + 1)],
+                                        rhs=vw[a, sh][:].bitcast(FP8X4), rhs_scale=vs[sh][4 * a:P, :], start=(a == 0), stop=(a == 1))
+                nc.scalar.activation(scaled[:, t, :], acc[:], ACT.Copy, scale=gain_t[:, b, t:t + 1])
+                nc.vector.tensor_scalar(held[:, t, :], scaled[:, t, :], low[:, b, t:t + 1], upp[:, b, t:t + 1], ALU.max, ALU.min)
+            woven = ring.tile([P, HALF * PACK], BF16, name="woven", align_bytes=64)
+            nc.vector.tensor_copy(woven[:].rearrange("p (c i t) -> p c t i", i=4, t=PACK), held[:].rearrange("p t (c i) -> p c t i", i=4))
+            hq[b, sh] = quantise(woven, "h%d%d" % (b, sh))
+
+        g2 = [keep.tile([P, S], F32, name="g2_%d" % t) for t in range(PACK)]
+        w3q = {}
+
+        def stage2(t, sh):
+            acc_b = psum.tile([P, HALF], F32, name="acc")
+            for b in range(2):
+                codes, scales = hq[b, sh]
+                nc.tensor.matmul_mx(out=acc_b[:], lhsT=w2wd[:, b, t, :].bitcast(FP4X4), lhsT_scale=w2sd[:, b, t, :],
+                                    rhs=codes[:].bitcast(FP8X4), rhs_scale=scales[:], start=(b == 0), stop=(b == 1))
+            acc_l = psum.tile([P, HALF], F32, name="acc")
+            for b in range(2):
+                codes, scales = hq[b, sh]
+                wc, ws = w3q[b]
+                nc.tensor.matmul_mx(out=acc_l[:], lhsT=wc[:, P * t:P * (t + 1)].bitcast(FP8X4), lhsT_scale=ws[:, P * t:P * (t + 1)],
+                                    rhs=codes[:].bitcast(FP8X4), rhs_scale=scales[:], start=(b == 0), stop=(b == 1))
+            bent = ring.tile([P, HALF], F32, name="bent", bufs=4)
+            nc.scalar.activation(bent[:], acc_b[:], ACT.Tanh)
+            nc.vector.tensor_tensor(g2[t][:, HALF * sh:HALF * (sh + 1)], acc_l[:], bent[:], ALU.add)
+
+        stage1(0, 0)
+        w1q[0, 1] = quantise(cast_weight(w1raw[0, 1], "w101", 0), "w101")
+        stage1(0, 1)
+        w1q[1, 1] = quantise(cast_weight(w1raw[1, 1], "w111", 64), "w111")
+        stage1(1, 0)
+        w3q[0] = quantise(cast_weight(w3raw[0], "w30", 0), "w30")
+        w3q[1] = quantise(cast_weight(w3raw[1], "w31", 64), "w31")
+        stage1(1, 1)
+        for t in range(PACK):
+            stage2(t, 0)
+
+        y = keep.tile([P, PACK, PAIRS], F32, name="y")
+        out_rows = out_0.rearrange("(p t) m -> p t m", t=PACK)
+        ycodes = keep.tile([P, PAIRS], U32, name="ycodes", align_bytes=64)
+        yscales = keep.tile([P, PAIRS], U8, name="yscales", align_bytes=64)
+
+        def contrast(t, m0, m1):
+            second = ring.tile([P, m1 - m0], F32, name="second")
+            diff = ring.tile([P, m1 - m0], F32, name="diff")
+            nc.vector.tensor_copy(second[:], g2[t][:].indirect(p2[:, m0 // 16:m1 // 16]))
+            nc.vector.tensor_tensor(diff[:], g2[t][:].indirect(p1[:, m0 // 16:m1 // 16]), second[:], ALU.subtract)
+            nc.vector.tensor_scalar(y[:, t, m0:m1], diff[:], base_t[:, t:t + 1], None, ALU.max)
+            nc.sync.dma_start(out_rows[:, t, m0:m1], y[:, t, m0:m1])
+
+        def planes(m0, m1, engine_copy):
+            ywoven = keep.tile([P, (m1 - m0) * PACK], BF16, name="ywoven%d" % m0, align_bytes=64)
+            engine_copy(ywoven[:].rearrange("p (c i t) -> p c t i", i=4, t=PACK), y[:, :, m0:m1].rearrange("p t (c i) -> p c t i", i=4))
+            nc.vector.quantize_mx(out=ycodes[:, m0:m1].bitcast(FP8X4), scales=yscales[:, m0:m1], in_=ywoven[:])
+            nc.sync.dma_start(out_1[0].rearrange("p m t -> p (m t)").bitcast(I32)[:, m0:m1], ycodes[:, m0:m1].bitcast(I32))
+
+        for t in range(PACK):
+            stage2(t, 1)
+            if t < PACK - 1:
+                contrast(t, 0, PAIRS)
+        contrast(PACK - 1, 0, PAIRS // 2)
+        contrast(PACK - 1, PAIRS // 2, PAIRS)
+        planes(0, PAIRS // 2, nc.scalar.copy)
+        planes(PAIRS // 2, PAIRS, nc.vector.tensor_copy)
+        for q in range(4):
+            queue = nc.scalar if q % 2 else nc.sync
+            queue.dma_start(out_2[0, 4 * q:4 * q + 4, :].bitcast(I32), yscales[32 * q:32 * q + 4, :].bitcast(I32))

@@ -20,7 +20,7 @@ P = 128
 PACK = 4
 PASS = 512
 HALF = 512
-STAGE_DT = F32
+STAGE_DT = BF16
 
 
 def tile_list_cork_end_contrast_kernel(tc, tab_words, tab_scales, offs, pos1, pos2, w1, lo, hi, gain,
@@ -38,18 +38,17 @@ def tile_list_cork_end_contrast_kernel(tc, tab_words, tab_scales, offs, pos1, po
         ts = keep.tile([P, T], U8, name="ts", align_bytes=64)
         w2w = keep.tile([P, 2, 2 * N], U8, name="w2w", align_bytes=64)
         w2s = keep.tile([P, 2, N], U8, name="w2s", align_bytes=64)
-        w1raw = {(a, b): keep.tile([P, PACK, PASS], F32, name="w1raw%d%d" % (a, b)) for a in range(2) for b in range(2)}
+        w1raw = {(a, b): keep.tile([P, PACK, PASS], F32, name="w1raw%d%d" % (a, b), tag="w1raw%d%d" % (a, b), align_bytes=64) for a in range(2) for b in range(2)}
         w3raw = [keep.tile([P, PACK, N], F32, name="w3raw%d" % b) for b in range(2)]
-        lo_t = keep.tile([P, 2, PACK], F32, name="lo_t")
-        hi_t = keep.tile([P, 2, PACK], F32, name="hi_t")
-        gain_t = keep.tile([P, 2, PACK], F32, name="gain_t")
+        lo_t = keep.tile([P, 2, 2 * PACK], F32, name="lo_t")
+        hi_t = keep.tile([P, 2, 2 * PACK], F32, name="hi_t")
+        gain_t = keep.tile([P, 2, 2 * PACK], F32, name="gain_t")
         base_t = keep.tile([P, PACK], F32, name="base_t")
 
         warm = keep.tile([P, 2], F32, name="warm")
         nc.vector.memset(ts[:].bitcast(I32), 0)
         nc.vector.memset(w2s[:].rearrange("p b n -> p (b n)").bitcast(I32), 0)
         nc.vector.memset(warm[:, 0:1], 0.0)
-        nc.scalar.activation(warm[:, 1:2], warm[:, 0:1], ACT.Tanh)
 
         def load_table(a):
             nc.sync.dma_start(tw[a][:], tab_words[a].rearrange("p t i -> p (t i)").bitcast(I32))
@@ -57,29 +56,30 @@ def tile_list_cork_end_contrast_kernel(tc, tab_words, tab_scales, offs, pos1, po
         def load_w1(a, b):
             nc.sync.dma_start(w1raw[a, b][:], w1[PASS * a:PASS * (a + 1), PASS * b:PASS * (b + 1)].rearrange("(p j) c -> p j c", j=PACK))
 
-        def load_vec(queue, src, dst):
-            queue.dma_start(dst[:], src.rearrange("(b p t) -> p b t", b=2, t=PACK))
+        def load_vec(src, dst):
+            nc.sync.dma_start(dst[:, :, 0:PACK], src.rearrange("(b p t) -> p b t", b=2, t=PACK))
 
+        nc.sync.dma_start(idx[:], offs)
+        nc.sync.dma_start(w2w[:].bitcast(I32), w2_words.rearrange("b p c -> p b c").bitcast(I32))
         load_table(0)
         for q in range(4):
             nc.sync.dma_start(ts[32 * q:32 * q + 8, :].bitcast(I32), tab_scales[:, 4 * q:4 * q + 4, :].bitcast(I32))
-        nc.sync.dma_start(idx[:], offs)
         load_w1(0, 0)
-        nc.sync.dma_start(w2w[:].bitcast(I32), w2_words.rearrange("b p c -> p b c").bitcast(I32))
         load_table(1)
-        for q in range(4):
-            nc.sync.dma_start(w2s[32 * q:32 * q + 4, :, :].bitcast(I32), w2_scales[:, 4 * q:4 * q + 4, :].rearrange("b r n -> r b n").bitcast(I32))
         load_w1(1, 0)
         for src, dst in ((gain, gain_t), (lo, lo_t), (hi, hi_t)):
-            load_vec(nc.sync, src, dst)
+            load_vec(src, dst)
         load_w1(0, 1)
         load_w1(1, 1)
+        for q in range(4):
+            nc.sync.dma_start(w2s[32 * q:32 * q + 4, :, :].bitcast(I32), w2_scales[:, 4 * q:4 * q + 4, :].rearrange("b r n -> r b n").bitcast(I32))
         for b in range(2):
             nc.sync.dma_start(w3raw[b][:], w3[PASS * b:PASS * (b + 1), :].rearrange("(p j) c -> p j c", j=PACK))
         nc.sync.dma_start(p1[:], pos1)
         nc.sync.dma_start(p2[:], pos2)
         nc.sync.dma_start(base_t[:], base.rearrange("(p t) -> p t", t=PACK))
 
+        nc.scalar.activation(warm[:, 1:2], warm[:, 0:1], ACT.Tanh)
         vw = {(a, sh): keep.tile([P, HALF], U32, name="vw%d%d" % (a, sh), align_bytes=64) for a in range(2) for sh in range(2)}
         vs = [keep.tile([P, HALF], U8, name="vs%d" % sh, align_bytes=64) for sh in range(2)]
 
@@ -89,8 +89,8 @@ def tile_list_cork_end_contrast_kernel(tc, tab_words, tab_scales, offs, pos1, po
         def gather_scales(sh):
             nc.vector.tensor_copy(vs[sh][:], ts[:].indirect(idx[:, 32 * sh:32 * (sh + 1)]))
 
-        def cast_weight(raw, name, m_vec):
-            grouped = ring.tile([P, PACK * PASS], BF16, name="grouped", bufs=3, align_bytes=64)
+        def cast_weight(raw, name, m_vec, slot):
+            grouped = keep.tile([P, PACK * PASS], BF16, name="g" + name, tag=slot, align_bytes=64)
             dst = grouped[:].rearrange("p (t m j) -> p m j t", t=PACK, j=PACK)
             src = raw[:].rearrange("p j (m t) -> p m j t", t=PACK)
             if m_vec > 0:
@@ -110,101 +110,148 @@ def tile_list_cork_end_contrast_kernel(tc, tab_words, tab_scales, offs, pos1, po
         eb = keep.tile([P, 2, PACK], F32, name="eb")
         low = keep.tile([P, 2, PACK], F32, name="low")
         upp = keep.tile([P, 2, PACK], F32, name="upp")
-        nc.vector.tensor_tensor(lo2[:], lo_t[:], hi_t[:], ALU.min)
-        nc.vector.tensor_tensor(eb[:], hi_t[:], gain_t[:], ALU.mult)
-        nc.vector.tensor_tensor(ea[:], lo2[:], gain_t[:], ALU.mult)
+        w2wd = keep.tile([P, 2, PACK, 2 * P], U8, name="w2wd", align_bytes=64)
+        nc.vector.tensor_copy(w2wd[:].rearrange("p b t (q e) -> p b q t e", e=2), w2w[:].rearrange("p b (q t e) -> p b q t e", t=PACK, e=2))
+        w1q = {}
+        w3q = {}
+        gather_words(0, 0)
+        gather_scales(0)
+        gather_words(0, 1)
+        gather_scales(1)
+        w1q[0, 0] = quantise(cast_weight(w1raw[0, 0], "w100", 0, "ga"), "w100")
+        gather_words(1, 0)
+        gather_words(1, 1)
+        w1q[1, 0] = quantise(cast_weight(w1raw[1, 0], "w110", 84, "gb"), "w110")
+
+        w2sd = keep.tile([P, 2, PACK, P], U8, name="w2sd", tag="w1raw10", align_bytes=64)
+        nc.vector.tensor_tensor(lo2[:], lo_t[:, :, 0:PACK], hi_t[:, :, 0:PACK], ALU.min)
+        nc.vector.tensor_tensor(eb[:], hi_t[:, :, 0:PACK], gain_t[:, :, 0:PACK], ALU.mult)
+        nc.vector.tensor_tensor(ea[:], lo2[:], gain_t[:, :, 0:PACK], ALU.mult)
         nc.vector.tensor_tensor(low[:], ea[:], eb[:], ALU.min)
         nc.vector.tensor_tensor(upp[:], ea[:], eb[:], ALU.max)
 
-        w1q = {}
-        gather_words(0, 0)
-        gather_words(0, 1)
-        gather_scales(0)
-        gather_scales(1)
-        g00 = cast_weight(w1raw[0, 0], "w100", 0)
-        w2wd = keep.tile([P, 2, PACK, 2 * P], U8, name="w2wd", align_bytes=64)
-        w2sd = keep.tile([P, 2, PACK, P], U8, name="w2sd", align_bytes=64)
-        nc.vector.tensor_copy(w2wd[:].rearrange("p b t (q e) -> p b q t e", e=2), w2w[:].rearrange("p b (q t e) -> p b q t e", t=PACK, e=2))
-        w1q[0, 0] = quantise(g00, "w100")
         nc.vector.tensor_copy(w2sd[:].rearrange("p b t q -> p b q t"), w2s[:].rearrange("p b (q t) -> p b q t", t=PACK))
-        gather_words(1, 0)
-        gather_words(1, 1)
-        w1q[1, 0] = quantise(cast_weight(w1raw[1, 0], "w110", 84), "w110")
+        hcodes = {(b, sh): keep.tile([P, HALF], U32, name="hc%d%d" % (b, sh), align_bytes=64) for b in range(2) for sh in range(2)}
+        hscales = {(b, sh): keep.tile([P, HALF], U8, name="hs%d%d" % (b, sh), align_bytes=64) for b in range(2) for sh in range(2)}
 
-        hq = {}
-
-        def stage1(b, sh):
-            scaled = ring.tile([P, PACK, HALF], STAGE_DT, name="scaled")
-            held = ring.tile([P, PACK, HALF], BF16, name="held")
+        def pores(b, sh, c0, c1, slots, between):
+            w = c1 - c0
+            per_bank = HALF // w
+            scaled = keep.tile([P, PACK, w], STAGE_DT, name="scaled", tag=slots[0], align_bytes=64)
+            held = keep.tile([P, PACK, w], BF16, name="held", tag=slots[1], align_bytes=64)
+            banks = []
             for t in range(PACK):
-                acc = psum.tile([P, HALF], F32, name="acc")
+                if t % per_bank == 0:
+                    banks.append(psum.tile([P, HALF], F32, name="acc"))
+                acc = banks[-1][:, w * (t % per_bank):w * (t % per_bank + 1)]
                 for a in range(2):
                     codes, scales = w1q[a, b]
-                    nc.tensor.matmul_mx(out=acc[:], lhsT=codes[:, P * t:P * (t + 1)].bitcast(FP8X4), lhsT_scale=scales[:, P * t:P * (t + 1)],
-                                        rhs=vw[a, sh][:].bitcast(FP8X4), rhs_scale=vs[sh][4 * a:P, :], start=(a == 0), stop=(a == 1))
-                nc.scalar.activation(scaled[:, t, :], acc[:], ACT.Copy, scale=gain_t[:, b, t:t + 1])
-                nc.vector.tensor_scalar(held[:, t, :], scaled[:, t, :], low[:, b, t:t + 1], upp[:, b, t:t + 1], ALU.max, ALU.min)
-            woven = ring.tile([P, HALF * PACK], BF16, name="woven", align_bytes=64)
+                    nc.tensor.matmul_mx(out=acc, lhsT=codes[:, P * t:P * (t + 1)].bitcast(FP8X4), lhsT_scale=scales[:, P * t:P * (t + 1)],
+                                        rhs=vw[a, sh][:, c0:c1].bitcast(FP8X4), rhs_scale=vs[sh][4 * a:P, c0:c1], start=(a == 0), stop=(a == 1))
+                if t % per_bank == per_bank - 1:
+                    for u in range(t + 1 - per_bank, t + 1):
+                        nc.scalar.activation(scaled[:, u, :], banks[-1][:, w * (u % per_bank):w * (u % per_bank + 1)], ACT.Copy, scale=gain_t[:, b, u:u + 1])
+                        nc.vector.tensor_scalar(held[:, u, :], scaled[:, u, :], low[:, b, u:u + 1], upp[:, b, u:u + 1], ALU.max, ALU.min)
+                        for call in between.get(u, ()):
+                            call()
+            woven = ring.tile([P, w * PACK], BF16, name="woven", align_bytes=64)
             nc.vector.tensor_copy(woven[:].rearrange("p (c i t) -> p c t i", i=4, t=PACK), held[:].rearrange("p t (c i) -> p c t i", i=4))
-            hq[b, sh] = quantise(woven, "h%d%d" % (b, sh))
+
+            def finish():
+                nc.vector.quantize_mx(out=hcodes[b, sh][:, c0:c1].bitcast(FP8X4), scales=hscales[b, sh][:, c0:c1], in_=woven[:])
+            return finish
 
         g2 = [keep.tile([P, S], F32, name="g2_%d" % t) for t in range(PACK)]
-        w3q = {}
 
-        def stage2(t, sh):
+        def scores(t, sh):
             acc_b = psum.tile([P, HALF], F32, name="acc")
             for b in range(2):
-                codes, scales = hq[b, sh]
                 nc.tensor.matmul_mx(out=acc_b[:], lhsT=w2wd[:, b, t, :].bitcast(FP4X4), lhsT_scale=w2sd[:, b, t, :],
-                                    rhs=codes[:].bitcast(FP8X4), rhs_scale=scales[:], start=(b == 0), stop=(b == 1))
+                                    rhs=hcodes[b, sh][:].bitcast(FP8X4), rhs_scale=hscales[b, sh][:], start=(b == 0), stop=(b == 1))
             acc_l = psum.tile([P, HALF], F32, name="acc")
             for b in range(2):
-                codes, scales = hq[b, sh]
                 wc, ws = w3q[b]
                 nc.tensor.matmul_mx(out=acc_l[:], lhsT=wc[:, P * t:P * (t + 1)].bitcast(FP8X4), lhsT_scale=ws[:, P * t:P * (t + 1)],
-                                    rhs=codes[:].bitcast(FP8X4), rhs_scale=scales[:], start=(b == 0), stop=(b == 1))
+                                    rhs=hcodes[b, sh][:].bitcast(FP8X4), rhs_scale=hscales[b, sh][:], start=(b == 0), stop=(b == 1))
             bent = ring.tile([P, HALF], F32, name="bent", bufs=4)
             nc.scalar.activation(bent[:], acc_b[:], ACT.Tanh)
             nc.vector.tensor_tensor(g2[t][:, HALF * sh:HALF * (sh + 1)], acc_l[:], bent[:], ALU.add)
 
-        stage1(0, 0)
-        w1q[0, 1] = quantise(cast_weight(w1raw[0, 1], "w101", 0), "w101")
-        stage1(0, 1)
-        w1q[1, 1] = quantise(cast_weight(w1raw[1, 1], "w111", 64), "w111")
-        stage1(1, 0)
-        w3q[0] = quantise(cast_weight(w3raw[0], "w30", 0), "w30")
-        w3q[1] = quantise(cast_weight(w3raw[1], "w31", 64), "w31")
-        stage1(1, 1)
-        for t in range(PACK):
-            stage2(t, 0)
+        staged = {}
+
+        def cast_later(key, raw, m_vec, slot):
+            return lambda: staged.setdefault(key, cast_weight(raw, key, m_vec, slot))
+
+        def quantise_later(key, table, at):
+            return lambda: table.setdefault(at, quantise(staged[key], key))
+
+        f = pores(0, 0, 0, 128, ("s0", "h0"), {})
+        cast_later("w101", w1raw[0, 1], 128, "s0")()
+        f = pores(0, 0, 128, 256, ("s1", "h1"), {0: [f], 1: [quantise_later("w101", w1q, (0, 1))]})
+        f = pores(0, 0, 256, 512, ("s2", "h0"), {0: [f], 3: [cast_later("w111", w1raw[1, 1], 64, "s1")]})
+        f = pores(0, 1, 0, 512, ("s0", "h1"), {0: [f, quantise_later("w111", w1q, (1, 1))], 3: [cast_later("w30", w3raw[0], 0, "s2")]})
+        f = pores(1, 0, 0, 512, ("s1", "h0"), {0: [f, quantise_later("w30", w3q, 0)], 3: [cast_later("w31", w3raw[1], 0, "s0")]})
+        f = pores(1, 1, 0, 256, ("ga", "gb"), {0: [f, quantise_later("w31", w3q, 1)]})
+        f = pores(1, 1, 256, 512, ("s2", "h1"), {0: [f]})
+        scores(0, 0)
+        f()
+        scores(1, 0)
+        scores(2, 0)
+        scores(0, 1)
 
         y = keep.tile([P, PACK, PAIRS], F32, name="y")
         out_rows = out_0.rearrange("(p t) m -> p t m", t=PACK)
         ycodes = keep.tile([P, PAIRS], U32, name="ycodes", align_bytes=64)
         yscales = keep.tile([P, PAIRS], U8, name="yscales", align_bytes=64)
+        second = {}
+        diff = {}
 
-        def contrast(t, m0, m1):
-            second = ring.tile([P, m1 - m0], F32, name="second")
-            diff = ring.tile([P, m1 - m0], F32, name="diff")
-            nc.vector.tensor_copy(second[:], g2[t][:].indirect(p2[:, m0 // 16:m1 // 16]))
-            nc.vector.tensor_tensor(diff[:], g2[t][:].indirect(p1[:, m0 // 16:m1 // 16]), second[:], ALU.subtract)
-            nc.vector.tensor_scalar(y[:, t, m0:m1], diff[:], base_t[:, t:t + 1], None, ALU.max)
+        def pick_second(t, m0, m1):
+            second[t, m0] = ring.tile([P, m1 - m0], F32, name="second")
+            nc.vector.tensor_copy(second[t, m0][:], g2[t][:].indirect(p2[:, m0 // 16:m1 // 16]))
+
+        def pick_first(t, m0, m1):
+            diff[t, m0] = ring.tile([P, m1 - m0], F32, name="diff")
+            nc.vector.tensor_tensor(diff[t, m0][:], g2[t][:].indirect(p1[:, m0 // 16:m1 // 16]), second[t, m0][:], ALU.subtract)
+
+        def floor(t, m0, m1):
+            nc.vector.tensor_scalar(y[:, t, m0:m1], diff[t, m0][:], base_t[:, t:t + 1], None, ALU.max)
             nc.sync.dma_start(out_rows[:, t, m0:m1], y[:, t, m0:m1])
 
-        def planes(m0, m1, engine_copy):
-            ywoven = keep.tile([P, (m1 - m0) * PACK], BF16, name="ywoven%d" % m0, align_bytes=64)
-            engine_copy(ywoven[:].rearrange("p (c i t) -> p c t i", i=4, t=PACK), y[:, :, m0:m1].rearrange("p t (c i) -> p c t i", i=4))
-            nc.vector.quantize_mx(out=ycodes[:, m0:m1].bitcast(FP8X4), scales=yscales[:, m0:m1], in_=ywoven[:])
+        ywoven = {}
+
+        def weave(m0, m1, engine_copy):
+            ywoven[m0] = keep.tile([P, (m1 - m0) * PACK], BF16, name="ywoven%d" % m0, align_bytes=64)
+            engine_copy(ywoven[m0][:].rearrange("p (c i t) -> p c t i", i=4, t=PACK), y[:, :, m0:m1].rearrange("p t (c i) -> p c t i", i=4))
+
+        def planes(m0, m1):
+            nc.vector.quantize_mx(out=ycodes[:, m0:m1].bitcast(FP8X4), scales=yscales[:, m0:m1], in_=ywoven[m0][:])
             nc.sync.dma_start(out_1[0].rearrange("p m t -> p (m t)").bitcast(I32)[:, m0:m1], ycodes[:, m0:m1].bitcast(I32))
 
-        for t in range(PACK):
-            stage2(t, 1)
-            if t < PACK - 1:
-                contrast(t, 0, PAIRS)
-        contrast(PACK - 1, 0, PAIRS // 2)
-        contrast(PACK - 1, PAIRS // 2, PAIRS)
-        planes(0, PAIRS // 2, nc.scalar.copy)
-        planes(PAIRS // 2, PAIRS, nc.vector.tensor_copy)
+        M = PAIRS
+        pick_second(0, 0, M)
+        scores(1, 1)
+        pick_first(0, 0, M)
+        pick_second(1, 0, M)
+        floor(0, 0, M)
+        scores(2, 1)
+        pick_first(1, 0, M)
+        pick_second(2, 0, M)
+        scores(3, 0)
+        floor(1, 0, M)
+        scores(3, 1)
+        pick_first(2, 0, M)
+        pick_second(3, 0, M // 2)
+        floor(2, 0, M)
+        pick_first(3, 0, M // 2)
+        pick_second(3, M // 2, M)
+        floor(3, 0, M // 2)
+        weave(0, M // 2, nc.scalar.copy)
+        pick_first(3, M // 2, M)
+        floor(3, M // 2, M)
+        weave(M // 2, M, nc.vector.tensor_copy)
+        planes(0, M // 2)
+        planes(M // 2, M)
         for q in range(4):
             queue = nc.scalar if q % 2 else nc.sync
             queue.dma_start(out_2[0, 4 * q:4 * q + 4, :].bitcast(I32), yscales[32 * q:32 * q + 4, :].bitcast(I32))

@@ -63,7 +63,9 @@ def tile_list_cork_end_contrast_kernel(tc, tab_words, tab_scales, offs, pos1, po
         nc.sync.dma_start(w2w[:].bitcast(I32), w2_words.rearrange("b p c -> p b c").bitcast(I32))
         load_table(0)
         for q in range(4):
-            nc.sync.dma_start(ts[32 * q:32 * q + 8, :].bitcast(I32), tab_scales[:, 4 * q:4 * q + 4, :].bitcast(I32))
+            nc.gpsimd.dma_start(ts[32 * q:32 * q + 8, :].bitcast(I32), tab_scales[:, 4 * q:4 * q + 4, :].bitcast(I32))
+        for q in range(4):
+            nc.gpsimd.dma_start(w2s[32 * q:32 * q + 4, :, :].bitcast(I32), w2_scales[:, 4 * q:4 * q + 4, :].rearrange("b r n -> r b n").bitcast(I32))
         load_w1(0, 0)
         load_table(1)
         load_w1(1, 0)
@@ -71,8 +73,6 @@ def tile_list_cork_end_contrast_kernel(tc, tab_words, tab_scales, offs, pos1, po
             load_vec(src, dst)
         load_w1(0, 1)
         load_w1(1, 1)
-        for q in range(4):
-            nc.sync.dma_start(w2s[32 * q:32 * q + 4, :, :].bitcast(I32), w2_scales[:, 4 * q:4 * q + 4, :].rearrange("b r n -> r b n").bitcast(I32))
         for b in range(2):
             nc.sync.dma_start(w3raw[b][:], w3[PASS * b:PASS * (b + 1), :].rearrange("(p j) c -> p j c", j=PACK))
         nc.sync.dma_start(p1[:], pos1)
@@ -91,8 +91,8 @@ def tile_list_cork_end_contrast_kernel(tc, tab_words, tab_scales, offs, pos1, po
 
         def cast_weight(raw, name, m_vec, slot):
             grouped = keep.tile([P, PACK * PASS], BF16, name="g" + name, tag=slot, align_bytes=64)
-            dst = grouped[:].rearrange("p (t m j) -> p m j t", t=PACK, j=PACK)
-            src = raw[:].rearrange("p j (m t) -> p m j t", t=PACK)
+            dst = grouped[:].rearrange("p (t m j) -> p m t j", t=PACK, j=PACK)
+            src = raw[:].rearrange("p j (m t) -> p m t j", t=PACK)
             if m_vec > 0:
                 nc.vector.tensor_copy(dst[:, 0:m_vec], src[:, 0:m_vec])
             if m_vec < P:
@@ -111,7 +111,7 @@ def tile_list_cork_end_contrast_kernel(tc, tab_words, tab_scales, offs, pos1, po
         low = keep.tile([P, 2, PACK], F32, name="low")
         upp = keep.tile([P, 2, PACK], F32, name="upp")
         w2wd = keep.tile([P, 2, PACK, 2 * P], U8, name="w2wd", align_bytes=64)
-        nc.vector.tensor_copy(w2wd[:].rearrange("p b t (q e) -> p b q t e", e=2), w2w[:].rearrange("p b (q t e) -> p b q t e", t=PACK, e=2))
+        nc.vector.tensor_copy(w2wd[:].rearrange("p b t (q e) -> p b t q e", e=2), w2w[:].rearrange("p b (q t e) -> p b t q e", t=PACK, e=2))
         w1q = {}
         w3q = {}
         gather_words(0, 0)
@@ -130,7 +130,7 @@ def tile_list_cork_end_contrast_kernel(tc, tab_words, tab_scales, offs, pos1, po
         nc.vector.tensor_tensor(low[:], ea[:], eb[:], ALU.min)
         nc.vector.tensor_tensor(upp[:], ea[:], eb[:], ALU.max)
 
-        nc.vector.tensor_copy(w2sd[:].rearrange("p b t q -> p b q t"), w2s[:].rearrange("p b (q t) -> p b q t", t=PACK))
+        nc.vector.tensor_copy(w2sd[:], w2s[:].rearrange("p b (q t) -> p b t q", t=PACK))
         hcodes = {(b, sh): keep.tile([P, HALF], U32, name="hc%d%d" % (b, sh), align_bytes=64) for b in range(2) for sh in range(2)}
         hscales = {(b, sh): keep.tile([P, HALF], U8, name="hs%d%d" % (b, sh), align_bytes=64) for b in range(2) for sh in range(2)}
 
@@ -155,7 +155,7 @@ def tile_list_cork_end_contrast_kernel(tc, tab_words, tab_scales, offs, pos1, po
                         for call in between.get(u, ()):
                             call()
             woven = ring.tile([P, w * PACK], BF16, name="woven", align_bytes=64)
-            nc.vector.tensor_copy(woven[:].rearrange("p (c i t) -> p c t i", i=4, t=PACK), held[:].rearrange("p t (c i) -> p c t i", i=4))
+            nc.vector.tensor_copy(woven[:].rearrange("p (c i t) -> p c t i", i=2, t=PACK), held[:].rearrange("p t (c i) -> p c t i", i=2))
 
             def finish():
                 nc.vector.quantize_mx(out=hcodes[b, sh][:, c0:c1].bitcast(FP8X4), scales=hscales[b, sh][:, c0:c1], in_=woven[:])
@@ -188,8 +188,9 @@ def tile_list_cork_end_contrast_kernel(tc, tab_words, tab_scales, offs, pos1, po
         f = pores(0, 0, 0, 128, ("s0", "h0"), {})
         cast_later("w101", w1raw[0, 1], 128, "s0")()
         f = pores(0, 0, 128, 256, ("s1", "h1"), {0: [f], 1: [quantise_later("w101", w1q, (0, 1))]})
-        f = pores(0, 0, 256, 512, ("s2", "h0"), {0: [f], 3: [cast_later("w111", w1raw[1, 1], 64, "s1")]})
-        f = pores(0, 1, 0, 512, ("s0", "h1"), {0: [f, quantise_later("w111", w1q, (1, 1))], 3: [cast_later("w30", w3raw[0], 0, "s2")]})
+        cast_later("w111", w1raw[1, 1], 128, "s1")()
+        f = pores(0, 0, 256, 512, ("s2", "h0"), {0: [f], 1: [quantise_later("w111", w1q, (1, 1))]})
+        f = pores(0, 1, 0, 512, ("s0", "h1"), {0: [f], 3: [cast_later("w30", w3raw[0], 0, "s2")]})
         f = pores(1, 0, 0, 512, ("s1", "h0"), {0: [f, quantise_later("w30", w3q, 0)], 3: [cast_later("w31", w3raw[1], 0, "s0")]})
         f = pores(1, 1, 0, 256, ("ga", "gb"), {0: [f, quantise_later("w31", w3q, 1)]})
         f = pores(1, 1, 256, 512, ("s2", "h1"), {0: [f]})
@@ -222,7 +223,7 @@ def tile_list_cork_end_contrast_kernel(tc, tab_words, tab_scales, offs, pos1, po
 
         def weave(m0, m1, engine_copy):
             ywoven[m0] = keep.tile([P, (m1 - m0) * PACK], BF16, name="ywoven%d" % m0, align_bytes=64)
-            engine_copy(ywoven[m0][:].rearrange("p (c i t) -> p c t i", i=4, t=PACK), y[:, :, m0:m1].rearrange("p t (c i) -> p c t i", i=4))
+            engine_copy(ywoven[m0][:].rearrange("p (c i t) -> p c t i", i=2, t=PACK), y[:, :, m0:m1].rearrange("p t (c i) -> p c t i", i=2))
 
         def planes(m0, m1):
             nc.vector.quantize_mx(out=ycodes[:, m0:m1].bitcast(FP8X4), scales=yscales[:, m0:m1], in_=ywoven[m0][:])

@@ -18,9 +18,18 @@ ACT = mybir.ActivationFunctionType
 
 P = 128
 PACK = 4
-PASS = 512
-HALF = 512
-STAGE_DT = BF16
+PASS = P * PACK
+PASSES = 2
+HALF = S // 2
+PER_COLUMN = 16
+QUADS = 4
+QUAD = P // QUADS
+ROWS = 4
+RUN = 4
+ALIGN = 64
+
+VECTOR_GROUPS_OPENING = 84
+VECTOR_GROUPS_LATER = 64
 
 
 def tile_list_cork_end_contrast_kernel(tc, tab_words, tab_scales, offs, pos1, pos2, w1, lo, hi, gain,
@@ -31,228 +40,195 @@ def tile_list_cork_end_contrast_kernel(tc, tab_words, tab_scales, offs, pos1, po
         ring = ctx.enter_context(tc.tile_pool(name="ring", bufs=2))
         psum = ctx.enter_context(tc.psum_pool(name="psum", bufs=8))
 
-        idx = keep.tile([P, S // 16], U16, name="idx")
-        p1 = keep.tile([P, PAIRS // 16], U16, name="p1")
-        p2 = keep.tile([P, PAIRS // 16], U16, name="p2")
-        tw = [keep.tile([P, T], I32, name="tw%d" % a, align_bytes=64) for a in range(2)]
-        ts = keep.tile([P, T], U8, name="ts", align_bytes=64)
-        w2w = keep.tile([P, 2, 2 * N], U8, name="w2w", align_bytes=64)
-        w2s = keep.tile([P, 2, N], U8, name="w2s", align_bytes=64)
-        w1raw = {(a, b): keep.tile([P, PACK, PASS], F32, name="w1raw%d%d" % (a, b), tag="w1raw%d%d" % (a, b), align_bytes=64) for a in range(2) for b in range(2)}
-        w3raw = [keep.tile([P, PACK, N], F32, name="w3raw%d" % b) for b in range(2)]
-        lo_t = keep.tile([P, 2, 2 * PACK], F32, name="lo_t")
-        hi_t = keep.tile([P, 2, 2 * PACK], F32, name="hi_t")
-        gain_t = keep.tile([P, 2, 2 * PACK], F32, name="gain_t")
-        base_t = keep.tile([P, PACK], F32, name="base_t")
+        idx = keep.tile([P, S // PER_COLUMN], U16, name="idx")
+        p1 = keep.tile([P, PAIRS // PER_COLUMN], U16, name="p1")
+        p2 = keep.tile([P, PAIRS // PER_COLUMN], U16, name="p2")
+        table_words = [keep.tile([P, T], I32, name="table_words%d" % a, align_bytes=ALIGN) for a in range(PASSES)]
+        table_scales = keep.tile([P, T], U8, name="table_scales", align_bytes=ALIGN)
+        w2_words_in = keep.tile([P, PASSES, 2 * N], U8, name="w2_words_in", align_bytes=ALIGN)
+        w2_scales_in = keep.tile([P, PASSES, N], U8, name="w2_scales_in", align_bytes=ALIGN)
+        w1_in = {(a, b): keep.tile([P, PACK, PASS], F32, name="w1_in%d%d" % (a, b)) for a in range(PASSES) for b in range(PASSES)}
+        w3_in = [keep.tile([P, PACK, N], F32, name="w3_in%d" % b) for b in range(PASSES)]
+        lo_in = keep.tile([P, PASSES, PACK], F32, name="lo_in")
+        hi_in = keep.tile([P, PASSES, PACK], F32, name="hi_in")
+        gain_in = keep.tile([P, PASSES, PACK], F32, name="gain_in")
+        base_in = keep.tile([P, PACK], F32, name="base_in")
 
-        warm = keep.tile([P, 2], F32, name="warm")
-        nc.vector.memset(ts[:].bitcast(I32), 0)
-        nc.vector.memset(w2s[:].rearrange("p b n -> p (b n)").bitcast(I32), 0)
-        nc.vector.memset(warm[:, 0:1], 0.0)
+        nc.vector.memset(table_scales[:].bitcast(I32), 0)
+        nc.vector.memset(w2_scales_in[:].rearrange("p b n -> p (b n)").bitcast(I32), 0)
 
         def load_table(a):
-            nc.sync.dma_start(tw[a][:], tab_words[a].rearrange("p t i -> p (t i)").bitcast(I32))
+            nc.sync.dma_start(table_words[a][:], tab_words[a].rearrange("p t i -> p (t i)").bitcast(I32))
 
         def load_w1(a, b):
-            nc.sync.dma_start(w1raw[a, b][:], w1[PASS * a:PASS * (a + 1), PASS * b:PASS * (b + 1)].rearrange("(p j) c -> p j c", j=PACK))
+            rows = w1[PASS * a:PASS * (a + 1), PASS * b:PASS * (b + 1)]
+            nc.sync.dma_start(w1_in[a, b][:], rows.rearrange("(p j) c -> p j c", j=PACK))
 
-        def load_vec(src, dst):
-            nc.sync.dma_start(dst[:, :, 0:PACK], src.rearrange("(b p t) -> p b t", b=2, t=PACK))
-
-        nc.sync.dma_start(idx[:], offs)
-        nc.sync.dma_start(w2w[:].bitcast(I32), w2_words.rearrange("b p c -> p b c").bitcast(I32))
         load_table(0)
-        for q in range(4):
-            nc.gpsimd.dma_start(ts[32 * q:32 * q + 8, :].bitcast(I32), tab_scales[:, 4 * q:4 * q + 4, :].bitcast(I32))
-        for q in range(4):
-            nc.gpsimd.dma_start(w2s[32 * q:32 * q + 4, :, :].bitcast(I32), w2_scales[:, 4 * q:4 * q + 4, :].rearrange("b r n -> r b n").bitcast(I32))
+        for q in range(QUADS):
+            nc.sync.dma_start(table_scales[QUAD * q:QUAD * q + PASSES * ROWS, :].bitcast(I32),
+                              tab_scales[:, ROWS * q:ROWS * (q + 1), :].bitcast(I32))
+        nc.sync.dma_start(idx[:], offs)
         load_w1(0, 0)
+        nc.sync.dma_start(w2_words_in[:].bitcast(I32), w2_words.rearrange("b p c -> p b c").bitcast(I32))
         load_table(1)
+        for q in range(QUADS):
+            nc.sync.dma_start(w2_scales_in[QUAD * q:QUAD * q + ROWS, :, :].bitcast(I32),
+                              w2_scales[:, ROWS * q:ROWS * (q + 1), :].rearrange("b r n -> r b n").bitcast(I32))
         load_w1(1, 0)
-        for src, dst in ((gain, gain_t), (lo, lo_t), (hi, hi_t)):
-            load_vec(src, dst)
+        for src, dst in ((gain, gain_in), (lo, lo_in), (hi, hi_in)):
+            nc.sync.dma_start(dst[:], src.rearrange("(b p t) -> p b t", b=PASSES, t=PACK))
         load_w1(0, 1)
         load_w1(1, 1)
-        for b in range(2):
-            nc.sync.dma_start(w3raw[b][:], w3[PASS * b:PASS * (b + 1), :].rearrange("(p j) c -> p j c", j=PACK))
+        for b in range(PASSES):
+            nc.sync.dma_start(w3_in[b][:], w3[PASS * b:PASS * (b + 1), :].rearrange("(p j) c -> p j c", j=PACK))
         nc.sync.dma_start(p1[:], pos1)
         nc.sync.dma_start(p2[:], pos2)
-        nc.sync.dma_start(base_t[:], base.rearrange("(p t) -> p t", t=PACK))
+        nc.sync.dma_start(base_in[:], base.rearrange("(p t) -> p t", t=PACK))
 
-        nc.scalar.activation(warm[:, 1:2], warm[:, 0:1], ACT.Tanh)
-        vw = {(a, sh): keep.tile([P, HALF], U32, name="vw%d%d" % (a, sh), align_bytes=64) for a in range(2) for sh in range(2)}
-        vs = [keep.tile([P, HALF], U8, name="vs%d" % sh, align_bytes=64) for sh in range(2)]
+        v_words = {(a, half): keep.tile([P, HALF], U32, name="v_words%d%d" % (a, half), align_bytes=ALIGN)
+                   for a in range(PASSES) for half in range(2)}
+        v_scales = [keep.tile([P, HALF], U8, name="v_scales%d" % half, align_bytes=ALIGN) for half in range(2)]
 
-        def gather_words(a, sh):
-            nc.vector.tensor_copy(vw[a, sh][:], tw[a][:].bitcast(U32).indirect(idx[:, 32 * sh:32 * (sh + 1)]))
+        def entries(tile, first, last):
+            return tile[:, first // PER_COLUMN:last // PER_COLUMN]
 
-        def gather_scales(sh):
-            nc.vector.tensor_copy(vs[sh][:], ts[:].indirect(idx[:, 32 * sh:32 * (sh + 1)]))
+        def gather_words(a, half):
+            window = table_words[a][:].bitcast(U32)
+            nc.vector.tensor_copy(v_words[a, half][:], window.indirect(entries(idx, HALF * half, HALF * (half + 1))))
 
-        def cast_weight(raw, name, m_vec, slot):
-            grouped = keep.tile([P, PACK * PASS], BF16, name="g" + name, tag=slot, align_bytes=64)
-            dst = grouped[:].rearrange("p (t m j) -> p m t j", t=PACK, j=PACK)
-            src = raw[:].rearrange("p j (m t) -> p m t j", t=PACK)
-            if m_vec > 0:
-                nc.vector.tensor_copy(dst[:, 0:m_vec], src[:, 0:m_vec])
-            if m_vec < P:
-                nc.scalar.copy(dst[:, m_vec:P], src[:, m_vec:P])
-            return grouped
+        def gather_scales(half):
+            nc.vector.tensor_copy(v_scales[half][:], table_scales[:].indirect(entries(idx, HALF * half, HALF * (half + 1))))
 
-        def quantise(grouped, name):
-            codes = keep.tile([P, PASS], U32, name="c" + name, align_bytes=64)
-            scales = keep.tile([P, PASS], U8, name="s" + name, align_bytes=64)
-            nc.vector.quantize_mx(out=codes[:].bitcast(FP8X4), scales=scales[:], in_=grouped[:])
-            return codes, scales
+        def round_and_deal(raw, vector_groups):
+            dealt = ring.tile([P, PACK * PASS], BF16, name="dealt", bufs=3, align_bytes=ALIGN)
+            dst = dealt[:].rearrange("p (t m j) -> p m j t", t=PACK, j=PACK)
+            src = raw[:].rearrange("p j (m t) -> p m j t", t=PACK)
+            if vector_groups > 0:
+                nc.vector.tensor_copy(dst[:, 0:vector_groups], src[:, 0:vector_groups])
+            nc.scalar.copy(dst[:, vector_groups:P], src[:, vector_groups:P])
+            return dealt
 
-        lo2 = keep.tile([P, 2, PACK], F32, name="lo2")
-        ea = keep.tile([P, 2, PACK], F32, name="ea")
-        eb = keep.tile([P, 2, PACK], F32, name="eb")
-        low = keep.tile([P, 2, PACK], F32, name="low")
-        upp = keep.tile([P, 2, PACK], F32, name="upp")
-        w2wd = keep.tile([P, 2, PACK, 2 * P], U8, name="w2wd", align_bytes=64)
-        nc.vector.tensor_copy(w2wd[:].rearrange("p b t (q e) -> p b t q e", e=2), w2w[:].rearrange("p b (q t e) -> p b t q e", t=PACK, e=2))
-        w1q = {}
-        w3q = {}
+        def quantise(values, name):
+            words = keep.tile([P, PASS], U32, name=name + "_words", align_bytes=ALIGN)
+            scales = keep.tile([P, PASS], U8, name=name + "_scales", align_bytes=ALIGN)
+            nc.vector.quantize_mx(out=words[:].bitcast(FP8X4), scales=scales[:], in_=values[:])
+            return words, scales
+
+        def weave(copy, woven, slices):
+            copy(woven.rearrange("p (c i t) -> p c t i", i=RUN, t=PACK), slices.rearrange("p t (c i) -> p c t i", i=RUN))
+
+        lo_eff = keep.tile([P, PASSES, PACK], F32, name="lo_eff")
+        gain_lo = keep.tile([P, PASSES, PACK], F32, name="gain_lo")
+        gain_hi = keep.tile([P, PASSES, PACK], F32, name="gain_hi")
+        lower = keep.tile([P, PASSES, PACK], F32, name="lower")
+        upper = keep.tile([P, PASSES, PACK], F32, name="upper")
+        nc.vector.tensor_tensor(lo_eff[:], lo_in[:], hi_in[:], ALU.min)
+        nc.vector.tensor_tensor(gain_hi[:], hi_in[:], gain_in[:], ALU.mult)
+        nc.vector.tensor_tensor(gain_lo[:], lo_eff[:], gain_in[:], ALU.mult)
+        nc.vector.tensor_tensor(lower[:], gain_lo[:], gain_hi[:], ALU.min)
+        nc.vector.tensor_tensor(upper[:], gain_lo[:], gain_hi[:], ALU.max)
+
+        w1_mx = {}
         gather_words(0, 0)
-        gather_scales(0)
         gather_words(0, 1)
+        gather_scales(0)
         gather_scales(1)
-        w1q[0, 0] = quantise(cast_weight(w1raw[0, 0], "w100", 0, "ga"), "w100")
+        w1_first = round_and_deal(w1_in[0, 0], 0)
+        w2_words_dealt = keep.tile([P, PASSES, PACK, 2 * P], U8, name="w2_words_dealt", align_bytes=ALIGN)
+        w2_scales_dealt = keep.tile([P, PASSES, PACK, P], U8, name="w2_scales_dealt", align_bytes=ALIGN)
+        nc.vector.tensor_copy(w2_words_dealt[:].rearrange("p b t (m e) -> p b m t e", e=2),
+                              w2_words_in[:].rearrange("p b (m t e) -> p b m t e", t=PACK, e=2))
+        w1_mx[0, 0] = quantise(w1_first, "w1_00")
+        nc.vector.tensor_copy(w2_scales_dealt[:].rearrange("p b t m -> p b m t"),
+                              w2_scales_in[:].rearrange("p b (m t) -> p b m t", t=PACK))
         gather_words(1, 0)
         gather_words(1, 1)
-        w1q[1, 0] = quantise(cast_weight(w1raw[1, 0], "w110", 84, "gb"), "w110")
+        w1_mx[1, 0] = quantise(round_and_deal(w1_in[1, 0], VECTOR_GROUPS_OPENING), "w1_10")
 
-        w2sd = keep.tile([P, 2, PACK, P], U8, name="w2sd", tag="w1raw10", align_bytes=64)
-        nc.vector.tensor_tensor(lo2[:], lo_t[:, :, 0:PACK], hi_t[:, :, 0:PACK], ALU.min)
-        nc.vector.tensor_tensor(eb[:], hi_t[:, :, 0:PACK], gain_t[:, :, 0:PACK], ALU.mult)
-        nc.vector.tensor_tensor(ea[:], lo2[:], gain_t[:, :, 0:PACK], ALU.mult)
-        nc.vector.tensor_tensor(low[:], ea[:], eb[:], ALU.min)
-        nc.vector.tensor_tensor(upp[:], ea[:], eb[:], ALU.max)
+        h_mx = {}
 
-        nc.vector.tensor_copy(w2sd[:], w2s[:].rearrange("p b (q t) -> p b t q", t=PACK))
-        hcodes = {(b, sh): keep.tile([P, HALF], U32, name="hc%d%d" % (b, sh), align_bytes=64) for b in range(2) for sh in range(2)}
-        hscales = {(b, sh): keep.tile([P, HALF], U8, name="hs%d%d" % (b, sh), align_bytes=64) for b in range(2) for sh in range(2)}
-
-        def pores(b, sh, c0, c1, slots, between):
-            w = c1 - c0
-            per_bank = HALF // w
-            scaled = keep.tile([P, PACK, w], STAGE_DT, name="scaled", tag=slots[0], align_bytes=64)
-            held = keep.tile([P, PACK, w], BF16, name="held", tag=slots[1], align_bytes=64)
-            banks = []
+        def make_h(b, half):
+            scaled = ring.tile([P, PACK, HALF], F32, name="scaled")
+            held = ring.tile([P, PACK, HALF], BF16, name="held")
             for t in range(PACK):
-                if t % per_bank == 0:
-                    banks.append(psum.tile([P, HALF], F32, name="acc"))
-                acc = banks[-1][:, w * (t % per_bank):w * (t % per_bank + 1)]
-                for a in range(2):
-                    codes, scales = w1q[a, b]
-                    nc.tensor.matmul_mx(out=acc, lhsT=codes[:, P * t:P * (t + 1)].bitcast(FP8X4), lhsT_scale=scales[:, P * t:P * (t + 1)],
-                                        rhs=vw[a, sh][:, c0:c1].bitcast(FP8X4), rhs_scale=vs[sh][4 * a:P, c0:c1], start=(a == 0), stop=(a == 1))
-                if t % per_bank == per_bank - 1:
-                    for u in range(t + 1 - per_bank, t + 1):
-                        nc.scalar.activation(scaled[:, u, :], banks[-1][:, w * (u % per_bank):w * (u % per_bank + 1)], ACT.Copy, scale=gain_t[:, b, u:u + 1])
-                        nc.vector.tensor_scalar(held[:, u, :], scaled[:, u, :], low[:, b, u:u + 1], upp[:, b, u:u + 1], ALU.max, ALU.min)
-                        for call in between.get(u, ()):
-                            call()
-            woven = ring.tile([P, w * PACK], BF16, name="woven", align_bytes=64)
-            nc.vector.tensor_copy(woven[:].rearrange("p (c i t) -> p c t i", i=2, t=PACK), held[:].rearrange("p t (c i) -> p c t i", i=2))
-
-            def finish():
-                nc.vector.quantize_mx(out=hcodes[b, sh][:, c0:c1].bitcast(FP8X4), scales=hscales[b, sh][:, c0:c1], in_=woven[:])
-            return finish
+                acc = psum.tile([P, HALF], F32, name="acc")
+                for a in range(PASSES):
+                    words, scales = w1_mx[a, b]
+                    nc.tensor.matmul_mx(out=acc[:], lhsT=words[:, P * t:P * (t + 1)].bitcast(FP8X4),
+                                        lhsT_scale=scales[:, P * t:P * (t + 1)],
+                                        rhs=v_words[a, half][:].bitcast(FP8X4), rhs_scale=v_scales[half][ROWS * a:P, :],
+                                        start=(a == 0), stop=(a == PASSES - 1))
+                nc.scalar.activation(scaled[:, t, :], acc[:], ACT.Copy, scale=gain_in[:, b, t:t + 1])
+                nc.vector.tensor_scalar(held[:, t, :], scaled[:, t, :], lower[:, b, t:t + 1], upper[:, b, t:t + 1],
+                                        ALU.max, ALU.min)
+            woven = ring.tile([P, HALF * PACK], BF16, name="woven", align_bytes=ALIGN)
+            weave(nc.vector.tensor_copy, woven[:], held[:])
+            h_mx[b, half] = quantise(woven, "h_%d%d" % (b, half))
 
         g2 = [keep.tile([P, S], F32, name="g2_%d" % t) for t in range(PACK)]
+        w3_mx = {}
 
-        def scores(t, sh):
-            acc_b = psum.tile([P, HALF], F32, name="acc")
-            for b in range(2):
-                nc.tensor.matmul_mx(out=acc_b[:], lhsT=w2wd[:, b, t, :].bitcast(FP4X4), lhsT_scale=w2sd[:, b, t, :],
-                                    rhs=hcodes[b, sh][:].bitcast(FP8X4), rhs_scale=hscales[b, sh][:], start=(b == 0), stop=(b == 1))
-            acc_l = psum.tile([P, HALF], F32, name="acc")
-            for b in range(2):
-                wc, ws = w3q[b]
-                nc.tensor.matmul_mx(out=acc_l[:], lhsT=wc[:, P * t:P * (t + 1)].bitcast(FP8X4), lhsT_scale=ws[:, P * t:P * (t + 1)],
-                                    rhs=hcodes[b, sh][:].bitcast(FP8X4), rhs_scale=hscales[b, sh][:], start=(b == 0), stop=(b == 1))
-            bent = ring.tile([P, HALF], F32, name="bent", bufs=4)
-            nc.scalar.activation(bent[:], acc_b[:], ACT.Tanh)
-            nc.vector.tensor_tensor(g2[t][:, HALF * sh:HALF * (sh + 1)], acc_l[:], bent[:], ALU.add)
+        def make_scores(t, half):
+            acc_bent = psum.tile([P, HALF], F32, name="acc")
+            for b in range(PASSES):
+                h_words, h_scales = h_mx[b, half]
+                nc.tensor.matmul_mx(out=acc_bent[:], lhsT=w2_words_dealt[:, b, t, :].bitcast(FP4X4),
+                                    lhsT_scale=w2_scales_dealt[:, b, t, :],
+                                    rhs=h_words[:].bitcast(FP8X4), rhs_scale=h_scales[:],
+                                    start=(b == 0), stop=(b == PASSES - 1))
+            acc_linear = psum.tile([P, HALF], F32, name="acc")
+            for b in range(PASSES):
+                h_words, h_scales = h_mx[b, half]
+                w3_words, w3_scales = w3_mx[b]
+                nc.tensor.matmul_mx(out=acc_linear[:], lhsT=w3_words[:, P * t:P * (t + 1)].bitcast(FP8X4),
+                                    lhsT_scale=w3_scales[:, P * t:P * (t + 1)],
+                                    rhs=h_words[:].bitcast(FP8X4), rhs_scale=h_scales[:],
+                                    start=(b == 0), stop=(b == PASSES - 1))
+            bent = ring.tile([P, HALF], F32, name="bent", bufs=PACK)
+            nc.scalar.activation(bent[:], acc_bent[:], ACT.Tanh)
+            nc.vector.tensor_tensor(g2[t][:, HALF * half:HALF * (half + 1)], acc_linear[:], bent[:], ALU.add)
 
-        staged = {}
-
-        def cast_later(key, raw, m_vec, slot):
-            return lambda: staged.setdefault(key, cast_weight(raw, key, m_vec, slot))
-
-        def quantise_later(key, table, at):
-            return lambda: table.setdefault(at, quantise(staged[key], key))
-
-        f = pores(0, 0, 0, 128, ("s0", "h0"), {})
-        cast_later("w101", w1raw[0, 1], 128, "s0")()
-        f = pores(0, 0, 128, 256, ("s1", "h1"), {0: [f], 1: [quantise_later("w101", w1q, (0, 1))]})
-        cast_later("w111", w1raw[1, 1], 128, "s1")()
-        f = pores(0, 0, 256, 512, ("s2", "h0"), {0: [f], 1: [quantise_later("w111", w1q, (1, 1))]})
-        f = pores(0, 1, 0, 512, ("s0", "h1"), {0: [f], 3: [cast_later("w30", w3raw[0], 0, "s2")]})
-        f = pores(1, 0, 0, 512, ("s1", "h0"), {0: [f, quantise_later("w30", w3q, 0)], 3: [cast_later("w31", w3raw[1], 0, "s0")]})
-        f = pores(1, 1, 0, 256, ("ga", "gb"), {0: [f, quantise_later("w31", w3q, 1)]})
-        f = pores(1, 1, 256, 512, ("s2", "h1"), {0: [f]})
-        scores(0, 0)
-        f()
-        scores(1, 0)
-        scores(2, 0)
-        scores(0, 1)
+        make_h(0, 0)
+        w1_mx[0, 1] = quantise(round_and_deal(w1_in[0, 1], 0), "w1_01")
+        make_h(0, 1)
+        w1_mx[1, 1] = quantise(round_and_deal(w1_in[1, 1], VECTOR_GROUPS_LATER), "w1_11")
+        make_h(1, 0)
+        w3_mx[0] = quantise(round_and_deal(w3_in[0], 0), "w3_0")
+        w3_mx[1] = quantise(round_and_deal(w3_in[1], VECTOR_GROUPS_LATER), "w3_1")
+        make_h(1, 1)
+        for t in range(PACK):
+            make_scores(t, 0)
 
         y = keep.tile([P, PACK, PAIRS], F32, name="y")
         out_rows = out_0.rearrange("(p t) m -> p t m", t=PACK)
-        ycodes = keep.tile([P, PAIRS], U32, name="ycodes", align_bytes=64)
-        yscales = keep.tile([P, PAIRS], U8, name="yscales", align_bytes=64)
-        second = {}
-        diff = {}
+        y_words = keep.tile([P, PAIRS], U32, name="y_words", align_bytes=ALIGN)
+        y_scales = keep.tile([P, PAIRS], U8, name="y_scales", align_bytes=ALIGN)
 
-        def pick_second(t, m0, m1):
-            second[t, m0] = ring.tile([P, m1 - m0], F32, name="second")
-            nc.vector.tensor_copy(second[t, m0][:], g2[t][:].indirect(p2[:, m0 // 16:m1 // 16]))
-
-        def pick_first(t, m0, m1):
-            diff[t, m0] = ring.tile([P, m1 - m0], F32, name="diff")
-            nc.vector.tensor_tensor(diff[t, m0][:], g2[t][:].indirect(p1[:, m0 // 16:m1 // 16]), second[t, m0][:], ALU.subtract)
-
-        def floor(t, m0, m1):
-            nc.vector.tensor_scalar(y[:, t, m0:m1], diff[t, m0][:], base_t[:, t:t + 1], None, ALU.max)
+        def contrast(t, m0, m1):
+            second = ring.tile([P, m1 - m0], F32, name="second")
+            diff = ring.tile([P, m1 - m0], F32, name="diff")
+            nc.vector.tensor_copy(second[:], g2[t][:].indirect(entries(p2, m0, m1)))
+            nc.vector.tensor_tensor(diff[:], g2[t][:].indirect(entries(p1, m0, m1)), second[:], ALU.subtract)
+            nc.vector.tensor_scalar(y[:, t, m0:m1], diff[:], base_in[:, t:t + 1], None, ALU.max)
             nc.sync.dma_start(out_rows[:, t, m0:m1], y[:, t, m0:m1])
 
-        ywoven = {}
+        def quantise_y(m0, m1, copy):
+            y_woven = keep.tile([P, (m1 - m0) * PACK], BF16, name="y_woven%d" % m0, align_bytes=ALIGN)
+            weave(copy, y_woven[:], y[:, :, m0:m1])
+            nc.vector.quantize_mx(out=y_words[:, m0:m1].bitcast(FP8X4), scales=y_scales[:, m0:m1], in_=y_woven[:])
+            nc.sync.dma_start(out_1[0].rearrange("p m t -> p (m t)").bitcast(I32)[:, m0:m1], y_words[:, m0:m1].bitcast(I32))
 
-        def weave(m0, m1, engine_copy):
-            ywoven[m0] = keep.tile([P, (m1 - m0) * PACK], BF16, name="ywoven%d" % m0, align_bytes=64)
-            engine_copy(ywoven[m0][:].rearrange("p (c i t) -> p c t i", i=2, t=PACK), y[:, :, m0:m1].rearrange("p t (c i) -> p c t i", i=2))
-
-        def planes(m0, m1):
-            nc.vector.quantize_mx(out=ycodes[:, m0:m1].bitcast(FP8X4), scales=yscales[:, m0:m1], in_=ywoven[m0][:])
-            nc.sync.dma_start(out_1[0].rearrange("p m t -> p (m t)").bitcast(I32)[:, m0:m1], ycodes[:, m0:m1].bitcast(I32))
-
-        M = PAIRS
-        pick_second(0, 0, M)
-        scores(1, 1)
-        pick_first(0, 0, M)
-        pick_second(1, 0, M)
-        floor(0, 0, M)
-        scores(2, 1)
-        pick_first(1, 0, M)
-        pick_second(2, 0, M)
-        scores(3, 0)
-        floor(1, 0, M)
-        scores(3, 1)
-        pick_first(2, 0, M)
-        pick_second(3, 0, M // 2)
-        floor(2, 0, M)
-        pick_first(3, 0, M // 2)
-        pick_second(3, M // 2, M)
-        floor(3, 0, M // 2)
-        weave(0, M // 2, nc.scalar.copy)
-        pick_first(3, M // 2, M)
-        floor(3, M // 2, M)
-        weave(M // 2, M, nc.vector.tensor_copy)
-        planes(0, M // 2)
-        planes(M // 2, M)
-        for q in range(4):
+        middle = PAIRS // 2
+        for t in range(PACK):
+            make_scores(t, 1)
+            if t < PACK - 1:
+                contrast(t, 0, PAIRS)
+        contrast(PACK - 1, 0, middle)
+        contrast(PACK - 1, middle, PAIRS)
+        quantise_y(0, middle, nc.scalar.copy)
+        quantise_y(middle, PAIRS, nc.vector.tensor_copy)
+        for q in range(QUADS):
             queue = nc.scalar if q % 2 else nc.sync
-            queue.dma_start(out_2[0, 4 * q:4 * q + 4, :].bitcast(I32), yscales[32 * q:32 * q + 4, :].bitcast(I32))
+            queue.dma_start(out_2[0, ROWS * q:ROWS * (q + 1), :].bitcast(I32),
+                            y_scales[QUAD * q:QUAD * q + ROWS, :].bitcast(I32))

from contextlib import ExitStack

import concourse.mybir as mybir

K, T, S, PAIRS, H, N = 1024, 4096, 1024, 512, 1024, 512
FLOPS = 2 * K * H * S + 2 * 2 * H * N * S

F32 = mybir.dt.float32
BF16 = mybir.dt.bfloat16
I32 = mybir.dt.int32
U32 = mybir.dt.uint32
U16 = mybir.dt.uint16
U8 = mybir.dt.uint8
FP8X4 = mybir.dt.float8_e4m3fn_x4
FP4X4 = mybir.dt.float4_e2m1fn_x4
ALU = mybir.AluOpType
ACT = mybir.ActivationFunctionType

P = 128
PACK = 4
PASS = P * PACK
PASSES = 2
HALF = S // 2
PER_COLUMN = 16
QUADS = 4
QUAD = P // QUADS
ROWS = 4
RUN = 4
ALIGN = 64

VECTOR_GROUPS_OPENING = 84
VECTOR_GROUPS_LATER = 64


def tile_list_cork_end_contrast_kernel(tc, tab_words, tab_scales, offs, pos1, pos2, w1, lo, hi, gain,
                                                 w2_words, w2_scales, w3, base, out_0, out_1, out_2):
    nc = tc.nc
    with ExitStack() as ctx:
        keep = ctx.enter_context(tc.tile_pool(name="keep", bufs=1))
        ring = ctx.enter_context(tc.tile_pool(name="ring", bufs=2))
        psum = ctx.enter_context(tc.psum_pool(name="psum", bufs=8))

        idx = keep.tile([P, S // PER_COLUMN], U16, name="idx")
        p1 = keep.tile([P, PAIRS // PER_COLUMN], U16, name="p1")
        p2 = keep.tile([P, PAIRS // PER_COLUMN], U16, name="p2")
        table_words = [keep.tile([P, T], I32, name="table_words%d" % a, align_bytes=ALIGN) for a in range(PASSES)]
        table_scales = keep.tile([P, T], U8, name="table_scales", align_bytes=ALIGN)
        w2_words_in = keep.tile([P, PASSES, 2 * N], U8, name="w2_words_in", align_bytes=ALIGN)
        w2_scales_in = keep.tile([P, PASSES, N], U8, name="w2_scales_in", align_bytes=ALIGN)
        w1_in = {(a, b): keep.tile([P, PACK, PASS], F32, name="w1_in%d%d" % (a, b)) for a in range(PASSES) for b in range(PASSES)}
        w3_in = [keep.tile([P, PACK, N], F32, name="w3_in%d" % b) for b in range(PASSES)]
        lo_in = keep.tile([P, PASSES, PACK], F32, name="lo_in")
        hi_in = keep.tile([P, PASSES, PACK], F32, name="hi_in")
        gain_in = keep.tile([P, PASSES, PACK], F32, name="gain_in")
        base_in = keep.tile([P, PACK], F32, name="base_in")

        nc.vector.memset(table_scales[:].bitcast(I32), 0)
        nc.vector.memset(w2_scales_in[:].rearrange("p b n -> p (b n)").bitcast(I32), 0)

        def load_table(a):
            nc.sync.dma_start(table_words[a][:], tab_words[a].rearrange("p t i -> p (t i)").bitcast(I32))

        def load_w1(a, b):
            rows = w1[PASS * a:PASS * (a + 1), PASS * b:PASS * (b + 1)]
            nc.sync.dma_start(w1_in[a, b][:], rows.rearrange("(p j) c -> p j c", j=PACK))

        load_table(0)
        for q in range(QUADS):
            nc.sync.dma_start(table_scales[QUAD * q:QUAD * q + PASSES * ROWS, :].bitcast(I32),
                              tab_scales[:, ROWS * q:ROWS * (q + 1), :].bitcast(I32))
        nc.sync.dma_start(idx[:], offs)
        load_w1(0, 0)
        nc.sync.dma_start(w2_words_in[:].bitcast(I32), w2_words.rearrange("b p c -> p b c").bitcast(I32))
        load_table(1)
        for q in range(QUADS):
            nc.sync.dma_start(w2_scales_in[QUAD * q:QUAD * q + ROWS, :, :].bitcast(I32),
                              w2_scales[:, ROWS * q:ROWS * (q + 1), :].rearrange("b r n -> r b n").bitcast(I32))
        load_w1(1, 0)
        for src, dst in ((gain, gain_in), (lo, lo_in), (hi, hi_in)):
            nc.sync.dma_start(dst[:], src.rearrange("(b p t) -> p b t", b=PASSES, t=PACK))
        load_w1(0, 1)
        load_w1(1, 1)
        for b in range(PASSES):
            nc.sync.dma_start(w3_in[b][:], w3[PASS * b:PASS * (b + 1), :].rearrange("(p j) c -> p j c", j=PACK))
        nc.sync.dma_start(p1[:], pos1)
        nc.sync.dma_start(p2[:], pos2)
        nc.sync.dma_start(base_in[:], base.rearrange("(p t) -> p t", t=PACK))

        v_words = {(a, half): keep.tile([P, HALF], U32, name="v_words%d%d" % (a, half), align_bytes=ALIGN)
                   for a in range(PASSES) for half in range(2)}
        v_scales = [keep.tile([P, HALF], U8, name="v_scales%d" % half, align_bytes=ALIGN) for half in range(2)]

        def entries(tile, first, last):
            return tile[:, first // PER_COLUMN:last // PER_COLUMN]

        def gather_words(a, half):
            window = table_words[a][:].bitcast(U32)
            nc.vector.tensor_copy(v_words[a, half][:], window.indirect(entries(idx, HALF * half, HALF * (half + 1))))

        def gather_scales(half):
            nc.vector.tensor_copy(v_scales[half][:], table_scales[:].indirect(entries(idx, HALF * half, HALF * (half + 1))))

        def round_and_deal(raw, vector_groups):
            dealt = ring.tile([P, PACK * PASS], BF16, name="dealt", bufs=3, align_bytes=ALIGN)
            dst = dealt[:].rearrange("p (t m j) -> p m j t", t=PACK, j=PACK)
            src = raw[:].rearrange("p j (m t) -> p m j t", t=PACK)
            if vector_groups > 0:
                nc.vector.tensor_copy(dst[:, 0:vector_groups], src[:, 0:vector_groups])
            nc.scalar.copy(dst[:, vector_groups:P], src[:, vector_groups:P])
            return dealt

        def quantise(values, name):
            words = keep.tile([P, PASS], U32, name=name + "_words", align_bytes=ALIGN)
            scales = keep.tile([P, PASS], U8, name=name + "_scales", align_bytes=ALIGN)
            nc.vector.quantize_mx(out=words[:].bitcast(FP8X4), scales=scales[:], in_=values[:])
            return words, scales

        def weave(copy, woven, slices):
            copy(woven.rearrange("p (c i t) -> p c t i", i=RUN, t=PACK), slices.rearrange("p t (c i) -> p c t i", i=RUN))

        lo_eff = keep.tile([P, PASSES, PACK], F32, name="lo_eff")
        gain_lo = keep.tile([P, PASSES, PACK], F32, name="gain_lo")
        gain_hi = keep.tile([P, PASSES, PACK], F32, name="gain_hi")
        lower = keep.tile([P, PASSES, PACK], F32, name="lower")
        upper = keep.tile([P, PASSES, PACK], F32, name="upper")
        nc.vector.tensor_tensor(lo_eff[:], lo_in[:], hi_in[:], ALU.min)
        nc.vector.tensor_tensor(gain_hi[:], hi_in[:], gain_in[:], ALU.mult)
        nc.vector.tensor_tensor(gain_lo[:], lo_eff[:], gain_in[:], ALU.mult)
        nc.vector.tensor_tensor(lower[:], gain_lo[:], gain_hi[:], ALU.min)
        nc.vector.tensor_tensor(upper[:], gain_lo[:], gain_hi[:], ALU.max)

        w1_mx = {}
        gather_words(0, 0)
        gather_words(0, 1)
        gather_scales(0)
        gather_scales(1)
        w1_first = round_and_deal(w1_in[0, 0], 0)
        w2_words_dealt = keep.tile([P, PASSES, PACK, 2 * P], U8, name="w2_words_dealt", align_bytes=ALIGN)
        w2_scales_dealt = keep.tile([P, PASSES, PACK, P], U8, name="w2_scales_dealt", align_bytes=ALIGN)
        nc.vector.tensor_copy(w2_words_dealt[:].rearrange("p b t (m e) -> p b m t e", e=2),
                              w2_words_in[:].rearrange("p b (m t e) -> p b m t e", t=PACK, e=2))
        w1_mx[0, 0] = quantise(w1_first, "w1_00")
        nc.vector.tensor_copy(w2_scales_dealt[:].rearrange("p b t m -> p b m t"),
                              w2_scales_in[:].rearrange("p b (m t) -> p b m t", t=PACK))
        gather_words(1, 0)
        gather_words(1, 1)
        w1_mx[1, 0] = quantise(round_and_deal(w1_in[1, 0], VECTOR_GROUPS_OPENING), "w1_10")

        h_mx = {}

        def make_h(b, half):
            scaled = ring.tile([P, PACK, HALF], F32, name="scaled")
            held = ring.tile([P, PACK, HALF], BF16, name="held")
            for t in range(PACK):
                acc = psum.tile([P, HALF], F32, name="acc")
                for a in range(PASSES):
                    words, scales = w1_mx[a, b]
                    nc.tensor.matmul_mx(out=acc[:], lhsT=words[:, P * t:P * (t + 1)].bitcast(FP8X4),
                                        lhsT_scale=scales[:, P * t:P * (t + 1)],
                                        rhs=v_words[a, half][:].bitcast(FP8X4), rhs_scale=v_scales[half][ROWS * a:P, :],
                                        start=(a == 0), stop=(a == PASSES - 1))
                nc.scalar.activation(scaled[:, t, :], acc[:], ACT.Copy, scale=gain_in[:, b, t:t + 1])
                nc.vector.tensor_scalar(held[:, t, :], scaled[:, t, :], lower[:, b, t:t + 1], upper[:, b, t:t + 1],
                                        ALU.max, ALU.min)
            woven = ring.tile([P, HALF * PACK], BF16, name="woven", align_bytes=ALIGN)
            weave(nc.vector.tensor_copy, woven[:], held[:])
            h_mx[b, half] = quantise(woven, "h_%d%d" % (b, half))

        g2 = [keep.tile([P, S], F32, name="g2_%d" % t) for t in range(PACK)]
        w3_mx = {}

        def make_scores(t, half):
            acc_bent = psum.tile([P, HALF], F32, name="acc")
            for b in range(PASSES):
                h_words, h_scales = h_mx[b, half]
                nc.tensor.matmul_mx(out=acc_bent[:], lhsT=w2_words_dealt[:, b, t, :].bitcast(FP4X4),
                                    lhsT_scale=w2_scales_dealt[:, b, t, :],
                                    rhs=h_words[:].bitcast(FP8X4), rhs_scale=h_scales[:],
                                    start=(b == 0), stop=(b == PASSES - 1))
            acc_linear = psum.tile([P, HALF], F32, name="acc")
            for b in range(PASSES):
                h_words, h_scales = h_mx[b, half]
                w3_words, w3_scales = w3_mx[b]
                nc.tensor.matmul_mx(out=acc_linear[:], lhsT=w3_words[:, P * t:P * (t + 1)].bitcast(FP8X4),
                                    lhsT_scale=w3_scales[:, P * t:P * (t + 1)],
                                    rhs=h_words[:].bitcast(FP8X4), rhs_scale=h_scales[:],
                                    start=(b == 0), stop=(b == PASSES - 1))
            bent = ring.tile([P, HALF], F32, name="bent", bufs=PACK)
            nc.scalar.activation(bent[:], acc_bent[:], ACT.Tanh)
            nc.vector.tensor_tensor(g2[t][:, HALF * half:HALF * (half + 1)], acc_linear[:], bent[:], ALU.add)

        make_h(0, 0)
        w1_mx[0, 1] = quantise(round_and_deal(w1_in[0, 1], 0), "w1_01")
        make_h(0, 1)
        w1_mx[1, 1] = quantise(round_and_deal(w1_in[1, 1], VECTOR_GROUPS_LATER), "w1_11")
        make_h(1, 0)
        w3_mx[0] = quantise(round_and_deal(w3_in[0], 0), "w3_0")
        w3_mx[1] = quantise(round_and_deal(w3_in[1], VECTOR_GROUPS_LATER), "w3_1")
        make_h(1, 1)
        for t in range(PACK):
            make_scores(t, 0)

        y = keep.tile([P, PACK, PAIRS], F32, name="y")
        out_rows = out_0.rearrange("(p t) m -> p t m", t=PACK)
        y_words = keep.tile([P, PAIRS], U32, name="y_words", align_bytes=ALIGN)
        y_scales = keep.tile([P, PAIRS], U8, name="y_scales", align_bytes=ALIGN)

        def contrast(t, m0, m1):
            second = ring.tile([P, m1 - m0], F32, name="second")
            diff = ring.tile([P, m1 - m0], F32, name="diff")
            nc.vector.tensor_copy(second[:], g2[t][:].indirect(entries(p2, m0, m1)))
            nc.vector.tensor_tensor(diff[:], g2[t][:].indirect(entries(p1, m0, m1)), second[:], ALU.subtract)
            nc.vector.tensor_scalar(y[:, t, m0:m1], diff[:], base_in[:, t:t + 1], None, ALU.max)
            nc.sync.dma_start(out_rows[:, t, m0:m1], y[:, t, m0:m1])

        def quantise_y(m0, m1, copy):
            y_woven = keep.tile([P, (m1 - m0) * PACK], BF16, name="y_woven%d" % m0, align_bytes=ALIGN)
            weave(copy, y_woven[:], y[:, :, m0:m1])
            nc.vector.quantize_mx(out=y_words[:, m0:m1].bitcast(FP8X4), scales=y_scales[:, m0:m1], in_=y_woven[:])
            nc.sync.dma_start(out_1[0].rearrange("p m t -> p (m t)").bitcast(I32)[:, m0:m1], y_words[:, m0:m1].bitcast(I32))

        middle = PAIRS // 2
        for t in range(PACK):
            make_scores(t, 1)
            if t < PACK - 1:
                contrast(t, 0, PAIRS)
        contrast(PACK - 1, 0, middle)
        contrast(PACK - 1, middle, PAIRS)
        quantise_y(0, middle, nc.scalar.copy)
        quantise_y(middle, PAIRS, nc.vector.tensor_copy)
        for q in range(QUADS):
            queue = nc.scalar if q % 2 else nc.sync
            queue.dma_start(out_2[0, ROWS * q:ROWS * (q + 1), :].bitcast(I32),
                            y_scales[QUAD * q:QUAD * q + ROWS, :].bitcast(I32))
